import numpy as np
import ml_dtypes


def mxq(x, axis, fmt="e4m3"):
    dtype, down = {"e4m3": (ml_dtypes.float8_e4m3fn, 7), "e5m2": (ml_dtypes.float8_e5m2, 14)}[fmt]
    v = np.moveaxis(np.asarray(x, np.float32).astype(ml_dtypes.bfloat16).astype(np.float64), axis, -1)
    blocks = v.reshape(v.shape[:-1] + (-1, 32))
    amax = np.abs(blocks).max(-1, keepdims=True)
    byte = np.maximum(np.where(amax > 0, np.frexp(amax)[1] - 1 + 127, 0) - down, 1)
    scale = np.exp2(byte - 127.0)
    codes = (blocks / scale).astype(np.float32).astype(dtype).astype(np.float64)
    return np.moveaxis((codes * scale).reshape(v.shape), -1, axis)


WIDE = False


def mx_kscale(k):
    if not WIDE:
        return np.ones(k)
    levels = np.array([10, -10, 5, -5, 0])
    if k % 512:
        return np.exp2(np.random.permutation(np.resize(levels, k // 32))).repeat(32)
    a = np.empty((k // 512, 16))
    for p in range(k // 512):
        a[p, :8] = np.random.permutation(np.resize(levels, 8))
        for g in range(8):
            far = levels[np.abs(levels - a[p, g]) >= 10]
            a[p, g + 8] = far[np.random.randint(len(far))]
    return np.exp2(a.ravel()).repeat(32)


def f64(x):
    return np.asarray(x).astype(np.float64)


def striped(idx):
    return np.tile(idx.reshape(-1, 16).T, (8, 1)).astype(np.uint16)


def unstriped(offs):
    return offs[:16].T.reshape(-1).astype(np.int64)


def relu2(v):
    return np.maximum(v, 0.0) ** 2


K, T, E, C, H, N = 512, 768, 6, 256, 1024, 256


def by_expert(wq, xq):
    return np.concatenate([wq[e].T @ xq[:, e * C:(e + 1) * C] for e in range(E)], axis=1)


def setup_inputs():
    n = np.random.standard_normal
    s = mx_kscale(K)[:, None]
    u = mx_kscale(H)
    first = np.random.permutation(np.repeat(np.arange(E), T // E))
    second = (first + 1 + np.random.permutation(np.repeat(np.arange(E - 1), -(-T // (E - 1)))[:T])) % E
    while np.bincount(second, minlength=E).max() != T // E:
        load = np.bincount(second, minlength=E); hi, lo = int(load.argmax()), int(load.argmin())
        t = np.flatnonzero((second == hi) & (first != lo))[0]; second[t] = lo
    slot_token = np.empty(E * C, np.int64); pos = np.empty((2, T), np.int64); fill = np.zeros(E, np.int64)
    place = np.stack([np.random.permutation(C) for _ in range(E)])
    for r, deal in enumerate((first, second)):
        for t in np.random.permutation(T):
            e = deal[t]; j = e * C + place[e, fill[e]]; fill[e] += 1; slot_token[j] = t; pos[r, t] = j
    g = np.random.uniform(0.2, 0.8, T)
    return {
        "xT": (n((K, T)) * s).astype(np.float32),
        "w1": (n((E, K, H)) / np.sqrt(K) / s[None] * u[None, None, :]).astype(np.float32),
        "w2": (n((E, H, N)) / np.sqrt(H) / u[None, :, None] ** 2).astype(np.float32),
        "gate": np.stack([np.tile(g, (N, 1)), np.tile(1.0 - g, (N, 1))]).astype(np.float32),
        "offs": striped(slot_token),
        "pos1": striped(pos[0]),
        "pos2": striped(pos[1]),
    }


def reference(xT, w1, w2, gate, offs, pos1, pos2):
    idx = unstriped(offs)
    xq = mxq(f64(xT)[:, idx], 0, "e4m3")
    h = relu2(by_expert(mxq(f64(w1), 1, "e4m3"), xq))
    y = by_expert(mxq(f64(w2), 1, "e4m3"), mxq(h, 0, "e4m3"))
    return f64(gate[0]) * y[:, unstriped(pos1)] + f64(gate[1]) * y[:, unstriped(pos2)]

@@ -1,0 +1,204 @@
+from contextlib import ExitStack
+
+import concourse.mybir as mybir
+
+K, T, E, C, H, N = 512, 768, 6, 256, 1024, 256
+FLOPS = 2 * E * C * (K * H + H * N)
+
+F32 = mybir.dt.float32
+BF16 = mybir.dt.bfloat16
+U32 = mybir.dt.uint32
+U16 = mybir.dt.uint16
+U8 = mybir.dt.uint8
+FP8X4 = mybir.dt.float8_e4m3fn_x4
+RELU = mybir.ActivationFunctionType.Relu
+SQUARE = mybir.ActivationFunctionType.Square
+MULT, ADD = mybir.AluOpType.mult, mybir.AluOpType.add
+
+P = 128
+X_CHUNKS = ((0, 512), (512, 768))
+SCALAR_M = (0, 128, 96, 96, 96, 64)
+
+
+def tile_routed_moe_kernel(tc, xT, w1, w2, gate, offs, pos1, pos2, out):
+    nc = tc.nc
+    with ExitStack() as ctx:
+        keep = ctx.enter_context(tc.tile_pool(name="keep", bufs=1))
+        raws = ctx.enter_context(tc.tile_pool(name="raws", bufs=3))
+        grouped = ctx.enter_context(tc.tile_pool(name="grouped", bufs=2))
+        codes = ctx.enter_context(tc.tile_pool(name="codes", bufs=2))
+        hidden = ctx.enter_context(tc.tile_pool(name="hidden", bufs=2))
+        psum1 = ctx.enter_context(tc.psum_pool(name="psum1", bufs=6))
+        psum2 = ctx.enter_context(tc.psum_pool(name="psum2", bufs=2))
+
+        offs_sb = keep.tile([P, E * C // 16], U16, name="offs_sb")
+        pos_sb = [keep.tile([P, T // 16], U16, name=f"pos{r}_sb") for r in range(2)]
+        x_raw = [keep.tile([P, 4, b - a], F32, name=f"x_raw{a}") for a, b in X_CHUNKS]
+        x_words = keep.tile([P, T], U32, name="x_words", align_bytes=64)
+        x_scales = keep.tile([P, T], U8, name="x_scales", align_bytes=64)
+        slot_codes = {}
+        gate_sb = [[keep.tile([P, T], F32, name=f"gate{r}{b}") for b in range(2)] for r in range(2)]
+        y_sb = [keep.tile([P, E * C], F32, name=f"y{b}") for b in range(2)]
+
+
+        w1_raw, w2_raw = {}, {}
+
+        def load_w1(e, parts=1, part=0):
+            if part == 0:
+                w1_raw[e] = raws.tile([P, 4, H], F32, name="w1_raw")
+            src = w1[e].rearrange("(p j) c -> p j c", j=4)
+            cols = slice(part * H // parts, (part + 1) * H // parts)
+            nc.sync.dma_start(w1_raw[e][:, :, cols], src[:, :, cols])
+
+        def load_w2(e):
+            w2_raw[e] = raws.tile([P, 2, 4, N], F32, name="w2_raw")
+            nc.sync.dma_start(w2_raw[e][:], w2[e].rearrange("(g p j) n -> p g j n", g=2, j=4))
+
+        x_grp = {}
+
+        def copy_x(i):
+            a, b = X_CHUNKS[i]
+            raw = x_raw[i]
+            x_grp[i] = keep.tile([P, b - a, 4], BF16, name=f"x_grp{a}", align_bytes=64)
+            half = (b - a) // 2
+            nc.vector.tensor_copy(out=x_grp[i][:, :half, :], in_=raw[:, :, :half].rearrange("p j t -> p t j"))
+            nc.scalar.copy(out=x_grp[i][:, half:, :], in_=raw[:, :, half:].rearrange("p j t -> p t j"))
+
+        def quant_x(i):
+            a, b = X_CHUNKS[i]
+            nc.vector.quantize_mx(out=x_words[:, a:b].bitcast(FP8X4), scales=x_scales[:, a:b],
+                                  in_=x_grp[i][:].rearrange("p t j -> p (t j)"))
+
+        def gather(e):
+            o = offs_sb[:, e * C // 16:(e + 1) * C // 16]
+            words = codes.tile([P, C], U32, name="slot_words", align_bytes=64)
+            scales = codes.tile([P, C], U8, name="slot_scales", align_bytes=64)
+            nc.vector.tensor_copy(out=words[:], in_=x_words[:].indirect(o))
+            nc.vector.tensor_copy(out=scales[:], in_=x_scales[:].indirect(o))
+            slot_codes[e] = (words, scales)
+
+        w1_grp, w1_codes, w2_grp, w2_codes, h_grp, h_codes = {}, {}, {}, {}, {}, {}
+
+        def copy_w1(e, g):
+            grp = grouped.tile([P, 4, 128, 4], BF16, name=f"w1_grp{g}", align_bytes=64)
+            dst = grp[:].rearrange("p t m j -> p m t j")
+            src = w1_raw[e][:, :, g * 512:(g + 1) * 512].rearrange("p j (m t) -> p m t j", t=4)
+            cut = SCALAR_M[e] if g == 1 else 0
+            if cut > 0:
+                nc.scalar.copy(out=dst[:, :cut], in_=src[:, :cut])
+            if cut < 128:
+                nc.vector.tensor_copy(out=dst[:, cut:], in_=src[:, cut:])
+            w1_grp[e, g] = grp
+
+        def quant_w1(e, g):
+            words = codes.tile([P, 512], U32, name=f"w1_words{g}", align_bytes=64)
+            scales = codes.tile([P, 512], U8, name=f"w1_scales{g}", align_bytes=64)
+            nc.vector.quantize_mx(out=words[:].bitcast(FP8X4), scales=scales[:],
+                                  in_=w1_grp[e, g][:].rearrange("p t m j -> p (t m j)"))
+            w1_codes[e, g] = (words, scales)
+
+        def copy_w2(e):
+            w2_grp[e] = grouped.tile([P, 2, N, 4], BF16, name="w2_grp", align_bytes=64)
+            nc.vector.tensor_copy(out=w2_grp[e][:], in_=w2_raw[e][:].rearrange("p g j n -> p g n j"))
+
+        def quant_w2(e):
+            words = codes.tile([P, 2 * N], U32, name="w2_words", align_bytes=64)
+            scales = codes.tile([P, 2 * N], U8, name="w2_scales", align_bytes=64)
+            nc.vector.quantize_mx(out=words[:].bitcast(FP8X4), scales=scales[:],
+                                  in_=w2_grp[e][:].rearrange("p g n j -> p (g n j)"))
+            w2_codes[e] = (words, scales)
+
+        relu_sb = {}
+
+        def layer1(e, g):
+            if g == 0:
+                relu_sb[e] = hidden.tile([P, 2, C, 4], F32, name="relu")
+                h_grp[e] = hidden.tile([P, 2, C, 4], BF16, name="h_grp", align_bytes=64)
+            words, scales = w1_codes[e, g]
+            sw, ss = slot_codes[e]
+            for s in range(2):
+                acc = psum1.tile([P, 4, 128], F32, name="acc1")
+                cols = slice(s * 128, (s + 1) * 128)
+                for t in range(4):
+                    rows = slice(t * 128, (t + 1) * 128)
+                    nc.tensor.matmul_mx(out=acc[:, t, :],
+                                        lhsT=words[:, rows].bitcast(FP8X4), lhsT_scale=scales[:, rows],
+                                        rhs=sw[:, cols].bitcast(FP8X4), rhs_scale=ss[:, cols],
+                                        start=True, stop=True)
+                nc.scalar.activation(out=relu_sb[e][:, g, cols, :], in_=acc[:].rearrange("p t c -> p c t"), func=RELU)
+            nc.scalar.activation(out=h_grp[e][:, g, :, :], in_=relu_sb[e][:, g, :, :], func=SQUARE)
+
+        def quant_h(e):
+            words = codes.tile([P, 2 * C], U32, name="h_words", align_bytes=64)
+            scales = codes.tile([P, 2 * C], U8, name="h_scales", align_bytes=64)
+            nc.vector.quantize_mx(out=words[:].bitcast(FP8X4), scales=scales[:],
+                                  in_=h_grp[e][:].rearrange("p g c t -> p (g c t)"))
+            h_codes[e] = (words, scales)
+
+        def layer2(e):
+            acc = psum2.tile([P, 2, C], F32, name="acc2")
+            ww, ws = w2_codes[e]
+            hw, hs = h_codes[e]
+            for b in range(2):
+                for g in range(2):
+                    rows = slice(g * N + b * 128, g * N + (b + 1) * 128)
+                    cols = slice(g * C, (g + 1) * C)
+                    nc.tensor.matmul_mx(out=acc[:, b, :],
+                                        lhsT=ww[:, rows].bitcast(FP8X4), lhsT_scale=ws[:, rows],
+                                        rhs=hw[:, cols].bitcast(FP8X4), rhs_scale=hs[:, cols],
+                                        start=(g == 0), stop=(g == 1))
+                nc.scalar.copy(out=y_sb[b][:, e * C:(e + 1) * C], in_=acc[:, b, :])
+
+        load_w1(0, 2, 0)
+        nc.sync.dma_start(offs_sb[:], offs)
+        for raw, (a, b) in zip(x_raw, X_CHUNKS):
+            nc.sync.dma_start(raw[:], xT.rearrange("(p j) t -> p j t", j=4)[:, :, a:b])
+        load_w1(0, 2, 1)
+        load_w1(1)
+        load_w2(0)
+        copy_w1(0, 0)
+        quant_w1(0, 0)
+        copy_x(0)
+        copy_x(1)
+        quant_x(0)
+        quant_x(1)
+        for e in range(E):
+            if e + 2 < E:
+                load_w1(e + 2)
+            if e == 0:
+                for r, src in enumerate((pos1, pos2)):
+                    nc.sync.dma_start(pos_sb[r][:], src)
+            if e > 0:
+                copy_w1(e, 0)
+            if e == 4:
+                load_w2(4)
+                load_w2(5)
+                for b in range(2):
+                    for r in range(2):
+                        nc.sync.dma_start(gate_sb[r][b][:], gate[r, b * 128:(b + 1) * 128, :])
+            elif e < 3:
+                load_w2(e + 1)
+            gather(e)
+            copy_w1(e, 1)
+            if e > 0:
+                quant_w1(e, 0)
+            layer1(e, 0)
+            if e > 0:
+                quant_h(e - 1)
+                layer2(e - 1)
+            quant_w1(e, 1)
+            layer1(e, 1)
+            copy_w2(e)
+            quant_w2(e)
+        quant_h(E - 1)
+        layer2(E - 1)
+
+        for b in range(2):
+            terms = []
+            for r in range(2):
+                term = hidden.tile([P, T], F32, name=f"term{r}")
+                nc.vector.tensor_tensor(out=term[:], in0=y_sb[b][:].indirect(pos_sb[r][:]), in1=gate_sb[r][b][:], op=MULT)
+                terms.append(term)
+            res = hidden.tile([P, T], F32, name="res")
+            nc.vector.tensor_tensor(out=res[:], in0=terms[0][:], in1=terms[1][:], op=ADD)
+            nc.sync.dma_start(out[b * 128:(b + 1) * 128, :], res[:])

@@ -17,17 +17,21 @@ MULT, ADD = mybir.AluOpType.mult, mybir.AluOpType.add
 
 P = 128
 X_CHUNKS = ((0, 512), (512, 768))
-SCALAR_M = (0, 128, 96, 96, 96, 64)
+W1_ON_SCALAR = ((0, 1), (1, 1), (2, 1), (3, 1), )
+W2_ON_SCALAR = ()
+Y_ENGINES = ["VS","VS","VS","VS","VS","VS"]
 
 
 def tile_routed_moe_kernel(tc, xT, w1, w2, gate, offs, pos1, pos2, out):
     nc = tc.nc
     with ExitStack() as ctx:
         keep = ctx.enter_context(tc.tile_pool(name="keep", bufs=1))
-        raws = ctx.enter_context(tc.tile_pool(name="raws", bufs=3))
+        raws1 = ctx.enter_context(tc.tile_pool(name="raws1", bufs=3))
+        raws2 = ctx.enter_context(tc.tile_pool(name="raws2", bufs=4))
         grouped = ctx.enter_context(tc.tile_pool(name="grouped", bufs=2))
         codes = ctx.enter_context(tc.tile_pool(name="codes", bufs=2))
         hidden = ctx.enter_context(tc.tile_pool(name="hidden", bufs=2))
+        results = ctx.enter_context(tc.tile_pool(name="results", bufs=2))
         psum1 = ctx.enter_context(tc.psum_pool(name="psum1", bufs=6))
         psum2 = ctx.enter_context(tc.psum_pool(name="psum2", bufs=2))
 
@@ -36,58 +40,67 @@ def tile_routed_moe_kernel(tc, xT, w1, w2, gate, offs, pos1, pos2, out):
         x_raw = [keep.tile([P, 4, b - a], F32, name=f"x_raw{a}") for a, b in X_CHUNKS]
         x_words = keep.tile([P, T], U32, name="x_words", align_bytes=64)
         x_scales = keep.tile([P, T], U8, name="x_scales", align_bytes=64)
-        slot_codes = {}
         gate_sb = [[keep.tile([P, T], F32, name=f"gate{r}{b}") for b in range(2)] for r in range(2)]
         y_sb = [keep.tile([P, E * C], F32, name=f"y{b}") for b in range(2)]
+        w1_raw, w2_raw, w1_grp, w2_grp, w1_codes, w2_codes = {}, {}, {}, {}, {}, {}
+        x_grp, slot_codes, relu_sb, h_grp, h_codes = {}, {}, {}, {}, {}
 
+        def load_offs():
+            nc.sync.dma_start(offs_sb[:], offs)
 
-        w1_raw, w2_raw = {}, {}
+        def load_pos():
+            for r, src in enumerate((pos1, pos2)):
+                nc.sync.dma_start(pos_sb[r][:], src)
 
-        def load_w1(e, parts=1, part=0):
-            if part == 0:
-                w1_raw[e] = raws.tile([P, 4, H], F32, name="w1_raw")
-            src = w1[e].rearrange("(p j) c -> p j c", j=4)
-            cols = slice(part * H // parts, (part + 1) * H // parts)
-            nc.sync.dma_start(w1_raw[e][:, :, cols], src[:, :, cols])
+        def load_x(i):
+            a, b = X_CHUNKS[i]
+            nc.sync.dma_start(x_raw[i][:], xT.rearrange("(p j) t -> p j t", j=4)[:, :, a:b])
+
+        def load_w1(e):
+            raw = raws1.tile([P, 4, H], F32, name="w1_raw")
+            nc.sync.dma_start(raw[:], w1[e].rearrange("(p j) c -> p j c", j=4))
+            for g in range(2):
+                w1_raw[e, g] = raw[:, :, g * 512:(g + 1) * 512]
+
+        def load_w1_half(e, g):
+            raw = raws2.tile([P, 4, 512], F32, name="w2_raw")
+            nc.sync.dma_start(raw[:], w1[e].rearrange("(p j) c -> p j c", j=4)[:, :, g * 512:(g + 1) * 512])
+            w1_raw[e, g] = raw[:]
 
         def load_w2(e):
-            w2_raw[e] = raws.tile([P, 2, 4, N], F32, name="w2_raw")
+            w2_raw[e] = raws2.tile([P, 2, 4, N], F32, name="w2_raw")
             nc.sync.dma_start(w2_raw[e][:], w2[e].rearrange("(g p j) n -> p g j n", g=2, j=4))
 
-        x_grp = {}
+        def load_gate(b):
+            for r in range(2):
+                nc.sync.dma_start(gate_sb[r][b][:], gate[r, b * 128:(b + 1) * 128, :])
 
         def copy_x(i):
             a, b = X_CHUNKS[i]
-            raw = x_raw[i]
             x_grp[i] = keep.tile([P, b - a, 4], BF16, name=f"x_grp{a}", align_bytes=64)
             half = (b - a) // 2
-            nc.vector.tensor_copy(out=x_grp[i][:, :half, :], in_=raw[:, :, :half].rearrange("p j t -> p t j"))
-            nc.scalar.copy(out=x_grp[i][:, half:, :], in_=raw[:, :, half:].rearrange("p j t -> p t j"))
+            nc.vector.tensor_copy(out=x_grp[i][:, :half, :], in_=x_raw[i][:, :, :half].rearrange("p j t -> p t j"))
+            nc.scalar.copy(out=x_grp[i][:, half:, :], in_=x_raw[i][:, :, half:].rearrange("p j t -> p t j"))
 
         def quant_x(i):
             a, b = X_CHUNKS[i]
             nc.vector.quantize_mx(out=x_words[:, a:b].bitcast(FP8X4), scales=x_scales[:, a:b],
                                   in_=x_grp[i][:].rearrange("p t j -> p (t j)"))
 
-        def gather(e):
-            o = offs_sb[:, e * C // 16:(e + 1) * C // 16]
-            words = codes.tile([P, C], U32, name="slot_words", align_bytes=64)
-            scales = codes.tile([P, C], U8, name="slot_scales", align_bytes=64)
+        def gather(e0, e1):
+            n = (e1 - e0) * C
+            o = offs_sb[:, e0 * C // 16:e1 * C // 16]
+            words = codes.tile([P, n], U32, name="slot_words", align_bytes=64)
+            scales = codes.tile([P, n], U8, name="slot_scales", align_bytes=64)
             nc.vector.tensor_copy(out=words[:], in_=x_words[:].indirect(o))
             nc.vector.tensor_copy(out=scales[:], in_=x_scales[:].indirect(o))
-            slot_codes[e] = (words, scales)
-
-        w1_grp, w1_codes, w2_grp, w2_codes, h_grp, h_codes = {}, {}, {}, {}, {}, {}
+            for e in range(e0, e1):
+                slot_codes[e] = (words, scales, (e - e0) * C)
 
         def copy_w1(e, g):
             grp = grouped.tile([P, 4, 128, 4], BF16, name=f"w1_grp{g}", align_bytes=64)
-            dst = grp[:].rearrange("p t m j -> p m t j")
-            src = w1_raw[e][:, :, g * 512:(g + 1) * 512].rearrange("p j (m t) -> p m t j", t=4)
-            cut = SCALAR_M[e] if g == 1 else 0
-            if cut > 0:
-                nc.scalar.copy(out=dst[:, :cut], in_=src[:, :cut])
-            if cut < 128:
-                nc.vector.tensor_copy(out=dst[:, cut:], in_=src[:, cut:])
+            copy = nc.scalar.copy if (e, g) in W1_ON_SCALAR else nc.vector.tensor_copy
+            copy(out=grp[:].rearrange("p t m j -> p m t j"), in_=w1_raw[e, g].rearrange("p j (m t) -> p m t j", t=4))
             w1_grp[e, g] = grp
 
         def quant_w1(e, g):
@@ -99,7 +112,8 @@ def tile_routed_moe_kernel(tc, xT, w1, w2, gate, offs, pos1, pos2, out):
 
         def copy_w2(e):
             w2_grp[e] = grouped.tile([P, 2, N, 4], BF16, name="w2_grp", align_bytes=64)
-            nc.vector.tensor_copy(out=w2_grp[e][:], in_=w2_raw[e][:].rearrange("p g j n -> p g n j"))
+            copy = nc.scalar.copy if e in W2_ON_SCALAR else nc.vector.tensor_copy
+            copy(out=w2_grp[e][:], in_=w2_raw[e][:].rearrange("p g j n -> p g n j"))
 
         def quant_w2(e):
             words = codes.tile([P, 2 * N], U32, name="w2_words", align_bytes=64)
@@ -108,97 +122,118 @@ def tile_routed_moe_kernel(tc, xT, w1, w2, gate, offs, pos1, pos2, out):
                                   in_=w2_grp[e][:].rearrange("p g n j -> p (g n j)"))
             w2_codes[e] = (words, scales)
 
-        relu_sb = {}
-
-        def layer1(e, g):
+        def mm1(e, g):
             if g == 0:
                 relu_sb[e] = hidden.tile([P, 2, C, 4], F32, name="relu")
                 h_grp[e] = hidden.tile([P, 2, C, 4], BF16, name="h_grp", align_bytes=64)
             words, scales = w1_codes[e, g]
-            sw, ss = slot_codes[e]
+            slot_words, slot_scales, first = slot_codes[e]
             for s in range(2):
                 acc = psum1.tile([P, 4, 128], F32, name="acc1")
-                cols = slice(s * 128, (s + 1) * 128)
+                cols = slice(first + s * 128, first + (s + 1) * 128)
                 for t in range(4):
                     rows = slice(t * 128, (t + 1) * 128)
                     nc.tensor.matmul_mx(out=acc[:, t, :],
                                         lhsT=words[:, rows].bitcast(FP8X4), lhsT_scale=scales[:, rows],
-                                        rhs=sw[:, cols].bitcast(FP8X4), rhs_scale=ss[:, cols],
+                                        rhs=slot_words[:, cols].bitcast(FP8X4), rhs_scale=slot_scales[:, cols],
                                         start=True, stop=True)
-                nc.scalar.activation(out=relu_sb[e][:, g, cols, :], in_=acc[:].rearrange("p t c -> p c t"), func=RELU)
-            nc.scalar.activation(out=h_grp[e][:, g, :, :], in_=relu_sb[e][:, g, :, :], func=SQUARE)
+                dst, src = relu_sb[e][:, g, s * 128:(s + 1) * 128, :], acc[:].rearrange("p t c -> p c t")
+                nc.scalar.activation(out=dst, in_=src, func=RELU)
 
-        def quant_h(e):
-            words = codes.tile([P, 2 * C], U32, name="h_words", align_bytes=64)
-            scales = codes.tile([P, 2 * C], U8, name="h_scales", align_bytes=64)
-            nc.vector.quantize_mx(out=words[:].bitcast(FP8X4), scales=scales[:],
-                                  in_=h_grp[e][:].rearrange("p g c t -> p (g c t)"))
-            h_codes[e] = (words, scales)
+        def square(e, g=None):
+            part = slice(0, 2) if g is None else slice(g, g + 1)
+            nc.scalar.activation(out=h_grp[e][:, part, :, :], in_=relu_sb[e][:, part, :, :], func=SQUARE)
 
-        def layer2(e):
+        def quant_h(e, g=None):
+            part = slice(0, 2) if g is None else slice(g, g + 1)
+            cols = slice(part.start * C, part.stop * C)
+            if e not in h_codes:
+                words = codes.tile([P, 2 * C], U32, name="h_words", align_bytes=64)
+                scales = codes.tile([P, 2 * C], U8, name="h_scales", align_bytes=64)
+                h_codes[e] = (words, scales)
+            words, scales = h_codes[e]
+            nc.vector.quantize_mx(out=words[:, cols].bitcast(FP8X4), scales=scales[:, cols],
+                                  in_=h_grp[e][:, part, :, :].rearrange("p g c t -> p (g c t)"))
+
+        def mm2(e):
             acc = psum2.tile([P, 2, C], F32, name="acc2")
-            ww, ws = w2_codes[e]
-            hw, hs = h_codes[e]
+            w_words, w_scales = w2_codes[e]
+            h_words, h_scales = h_codes[e]
             for b in range(2):
                 for g in range(2):
                     rows = slice(g * N + b * 128, g * N + (b + 1) * 128)
                     cols = slice(g * C, (g + 1) * C)
                     nc.tensor.matmul_mx(out=acc[:, b, :],
-                                        lhsT=ww[:, rows].bitcast(FP8X4), lhsT_scale=ws[:, rows],
-                                        rhs=hw[:, cols].bitcast(FP8X4), rhs_scale=hs[:, cols],
+                                        lhsT=w_words[:, rows].bitcast(FP8X4), lhsT_scale=w_scales[:, rows],
+                                        rhs=h_words[:, cols].bitcast(FP8X4), rhs_scale=h_scales[:, cols],
                                         start=(g == 0), stop=(g == 1))
-                nc.scalar.copy(out=y_sb[b][:, e * C:(e + 1) * C], in_=acc[:, b, :])
+                copy = nc.scalar.copy if Y_ENGINES[e][b] == "S" else nc.vector.tensor_copy
+                copy(out=y_sb[b][:, e * C:(e + 1) * C], in_=acc[:, b, :])
 
-        load_w1(0, 2, 0)
-        nc.sync.dma_start(offs_sb[:], offs)
-        for raw, (a, b) in zip(x_raw, X_CHUNKS):
-            nc.sync.dma_start(raw[:], xT.rearrange("(p j) t -> p j t", j=4)[:, :, a:b])
-        load_w1(0, 2, 1)
+        def combine(b):
+            terms = []
+            for r in range(2):
+                term = results.tile([P, T], F32, name=f"term{r}")
+                nc.vector.tensor_tensor(out=term[:], in0=y_sb[b][:].indirect(pos_sb[r][:]), in1=gate_sb[r][b][:], op=MULT)
+                terms.append(term)
+            res = results.tile([P, T], F32, name="res")
+            nc.vector.tensor_tensor(out=res[:], in0=terms[0][:], in1=terms[1][:], op=ADD)
+            nc.sync.dma_start(out[b * 128:(b + 1) * 128, :], res[:])
+
+        load_offs()
+        load_x(0)
+        load_x(1)
+        load_w1_half(0, 0)
+        load_w1_half(0, 1)
         load_w1(1)
         load_w2(0)
-        copy_w1(0, 0)
-        quant_w1(0, 0)
+        load_w1(2)
         copy_x(0)
         copy_x(1)
         quant_x(0)
         quant_x(1)
+        copy_w1(0, 0)
+        quant_w1(0, 0)
+        gather(0, 1)
         for e in range(E):
-            if e + 2 < E:
-                load_w1(e + 2)
-            if e == 0:
-                for r, src in enumerate((pos1, pos2)):
-                    nc.sync.dma_start(pos_sb[r][:], src)
             if e > 0:
                 copy_w1(e, 0)
-            if e == 4:
-                load_w2(4)
-                load_w2(5)
-                for b in range(2):
-                    for r in range(2):
-                        nc.sync.dma_start(gate_sb[r][b][:], gate[r, b * 128:(b + 1) * 128, :])
-            elif e < 3:
-                load_w2(e + 1)
-            gather(e)
             copy_w1(e, 1)
+            if e + 3 < E:
+                load_w1(e + 3)
+            if e == 1:
+                load_pos()
+            if e < 3:
+                load_w2(e + 1)
+            if e == 3:
+                load_w2(4)
+            if e == 4:
+                load_w2(5)
+                load_gate(0)
+                load_gate(1)
+            if e in (1, 3):
+                gather(e, e + 2)
+            if e == 5:
+                gather(5, 6)
             if e > 0:
                 quant_w1(e, 0)
-            layer1(e, 0)
+            mm1(e, 0)
+            if e > 1:
+                mm2(e - 2)
             if e > 0:
                 quant_h(e - 1)
-                layer2(e - 1)
             quant_w1(e, 1)
-            layer1(e, 1)
+            mm1(e, 1)
+            if e < 5:
+                square(e)
+            else:
+                square(e, 0)
+                square(e, 1)
             copy_w2(e)
             quant_w2(e)
-        quant_h(E - 1)
-        layer2(E - 1)
-
-        for b in range(2):
-            terms = []
-            for r in range(2):
-                term = hidden.tile([P, T], F32, name=f"term{r}")
-                nc.vector.tensor_tensor(out=term[:], in0=y_sb[b][:].indirect(pos_sb[r][:]), in1=gate_sb[r][b][:], op=MULT)
-                terms.append(term)
-            res = hidden.tile([P, T], F32, name="res")
-            nc.vector.tensor_tensor(out=res[:], in0=terms[0][:], in1=terms[1][:], op=ADD)
-            nc.sync.dma_start(out[b * 128:(b + 1) * 128, :], res[:])
+        mm2(4)
+        quant_h(5, 0)
+        quant_h(5, 1)
+        mm2(5)
+        combine(0)
+        combine(1)

@@ -16,20 +16,24 @@ SQUARE = mybir.ActivationFunctionType.Square
 MULT, ADD = mybir.AluOpType.mult, mybir.AluOpType.add
 
 P = 128
-X_CHUNKS = ((0, 512), (512, 768))
-W1_ON_SCALAR = ((0, 1), (1, 1), (2, 1), (3, 1), )
-W2_ON_SCALAR = ()
-Y_ENGINES = ["VS","VS","VS","VS","VS","VS"]
+X_CHUNK = 256
+W1_ENGINES = ["SS","VV","V","V","SS","VS"]
+W2_ENGINES = ["V","V","V"]
+VECTOR_RELU = ((2, 1, 0), (2, 1, 1), (1, 1, 0), (1, 1, 1), (3, 1, 1), (1, 0, 0), )
+Y_ENGINES = ["SS","VS","SV","SS","SS","VV"]
 
 
 def tile_routed_moe_kernel(tc, xT, w1, w2, gate, offs, pos1, pos2, out):
     nc = tc.nc
     with ExitStack() as ctx:
         keep = ctx.enter_context(tc.tile_pool(name="keep", bufs=1))
-        raws1 = ctx.enter_context(tc.tile_pool(name="raws1", bufs=3))
-        raws2 = ctx.enter_context(tc.tile_pool(name="raws2", bufs=4))
-        grouped = ctx.enter_context(tc.tile_pool(name="grouped", bufs=2))
-        codes = ctx.enter_context(tc.tile_pool(name="codes", bufs=2))
+        raws = ctx.enter_context(tc.tile_pool(name="raws", bufs=3))
+        grouped1 = ctx.enter_context(tc.tile_pool(name="grouped1", bufs=3))
+        grouped2 = ctx.enter_context(tc.tile_pool(name="grouped2", bufs=1))
+        w1_pool = ctx.enter_context(tc.tile_pool(name="w1_pool", bufs=4))
+        w2_pool = ctx.enter_context(tc.tile_pool(name="w2_pool", bufs=3))
+        slots = ctx.enter_context(tc.tile_pool(name="slots", bufs=3))
+        hcodes = ctx.enter_context(tc.tile_pool(name="hcodes", bufs=3))
         hidden = ctx.enter_context(tc.tile_pool(name="hidden", bufs=2))
         results = ctx.enter_context(tc.tile_pool(name="results", bufs=2))
         psum1 = ctx.enter_context(tc.psum_pool(name="psum1", bufs=6))
@@ -37,13 +41,22 @@ def tile_routed_moe_kernel(tc, xT, w1, w2, gate, offs, pos1, pos2, out):
 
         offs_sb = keep.tile([P, E * C // 16], U16, name="offs_sb")
         pos_sb = [keep.tile([P, T // 16], U16, name=f"pos{r}_sb") for r in range(2)]
-        x_raw = [keep.tile([P, 4, b - a], F32, name=f"x_raw{a}") for a, b in X_CHUNKS]
+        x_raw = [keep.tile([P, 4, X_CHUNK], F32, name=f"x_raw{i}") for i in range(3)]
         x_words = keep.tile([P, T], U32, name="x_words", align_bytes=64)
         x_scales = keep.tile([P, T], U8, name="x_scales", align_bytes=64)
         gate_sb = [[keep.tile([P, T], F32, name=f"gate{r}{b}") for b in range(2)] for r in range(2)]
         y_sb = [keep.tile([P, E * C], F32, name=f"y{b}") for b in range(2)]
         w1_raw, w2_raw, w1_grp, w2_grp, w1_codes, w2_codes = {}, {}, {}, {}, {}, {}
         x_grp, slot_codes, relu_sb, h_grp, h_codes = {}, {}, {}, {}, {}
+
+        def copy_on(engine, dst, src):
+            if engine == "S":
+                nc.scalar.copy(out=dst, in_=src)
+            else:
+                nc.vector.tensor_copy(out=dst, in_=src)
+
+        def quantize(words, scales, src):
+            nc.vector.quantize_mx(out=words.bitcast(FP8X4), scales=scales, in_=src)
 
         def load_offs():
             nc.sync.dma_start(offs_sb[:], offs)
@@ -53,122 +66,136 @@ def tile_routed_moe_kernel(tc, xT, w1, w2, gate, offs, pos1, pos2, out):
                 nc.sync.dma_start(pos_sb[r][:], src)
 
         def load_x(i):
-            a, b = X_CHUNKS[i]
-            nc.sync.dma_start(x_raw[i][:], xT.rearrange("(p j) t -> p j t", j=4)[:, :, a:b])
+            nc.sync.dma_start(x_raw[i][:], xT.rearrange("(p j) t -> p j t", j=4)[:, :, i * X_CHUNK:(i + 1) * X_CHUNK])
 
         def load_w1(e):
-            raw = raws1.tile([P, 4, H], F32, name="w1_raw")
+            raw = raws.tile([P, 4, H], F32, name="raw")
             nc.sync.dma_start(raw[:], w1[e].rearrange("(p j) c -> p j c", j=4))
-            for g in range(2):
-                w1_raw[e, g] = raw[:, :, g * 512:(g + 1) * 512]
+            w1_raw[e] = [raw[:]]
 
         def load_w1_half(e, g):
-            raw = raws2.tile([P, 4, 512], F32, name="w2_raw")
+            raw = keep.tile([P, 4, 512], F32, name=f"w1_half{g}")
             nc.sync.dma_start(raw[:], w1[e].rearrange("(p j) c -> p j c", j=4)[:, :, g * 512:(g + 1) * 512])
-            w1_raw[e, g] = raw[:]
+            w1_raw.setdefault(e, []).append(raw[:])
 
-        def load_w2(e):
-            w2_raw[e] = raws2.tile([P, 2, 4, N], F32, name="w2_raw")
-            nc.sync.dma_start(w2_raw[e][:], w2[e].rearrange("(g p j) n -> p g j n", g=2, j=4))
+        def load_w2(i):
+            w2_raw[i] = raws.tile([P, 4, 4, N], F32, name="raw")
+            nc.sync.dma_start(w2_raw[i][:], w2[2 * i:2 * i + 2].rearrange("e (g p j) n -> p (e g) j n", g=2, j=4))
 
         def load_gate(b):
             for r in range(2):
                 nc.sync.dma_start(gate_sb[r][b][:], gate[r, b * 128:(b + 1) * 128, :])
 
-        def copy_x(i):
-            a, b = X_CHUNKS[i]
-            x_grp[i] = keep.tile([P, b - a, 4], BF16, name=f"x_grp{a}", align_bytes=64)
-            half = (b - a) // 2
-            nc.vector.tensor_copy(out=x_grp[i][:, :half, :], in_=x_raw[i][:, :, :half].rearrange("p j t -> p t j"))
-            nc.scalar.copy(out=x_grp[i][:, half:, :], in_=x_raw[i][:, :, half:].rearrange("p j t -> p t j"))
+        def copy_x(i, how):
+            x_grp[i] = keep.tile([P, X_CHUNK, 4], BF16, name=f"x_grp{i}", align_bytes=64)
+            src = x_raw[i][:].rearrange("p j t -> p t j")
+            if how == "B":
+                half = X_CHUNK // 2
+                copy_on("V", x_grp[i][:, :half, :], src[:, :half, :])
+                copy_on("S", x_grp[i][:, half:, :], src[:, half:, :])
+            else:
+                copy_on(how, x_grp[i][:], src)
 
         def quant_x(i):
-            a, b = X_CHUNKS[i]
-            nc.vector.quantize_mx(out=x_words[:, a:b].bitcast(FP8X4), scales=x_scales[:, a:b],
-                                  in_=x_grp[i][:].rearrange("p t j -> p (t j)"))
+            cols = slice(i * X_CHUNK, (i + 1) * X_CHUNK)
+            quantize(x_words[:, cols], x_scales[:, cols], x_grp[i][:].rearrange("p t j -> p (t j)"))
 
         def gather(e0, e1):
             n = (e1 - e0) * C
             o = offs_sb[:, e0 * C // 16:e1 * C // 16]
-            words = codes.tile([P, n], U32, name="slot_words", align_bytes=64)
-            scales = codes.tile([P, n], U8, name="slot_scales", align_bytes=64)
+            words = slots.tile([P, n], U32, name="slot_words", align_bytes=64)
+            scales = slots.tile([P, n], U8, name="slot_scales", align_bytes=64)
             nc.vector.tensor_copy(out=words[:], in_=x_words[:].indirect(o))
             nc.vector.tensor_copy(out=scales[:], in_=x_scales[:].indirect(o))
             for e in range(e0, e1):
                 slot_codes[e] = (words, scales, (e - e0) * C)
 
-        def copy_w1(e, g):
-            grp = grouped.tile([P, 4, 128, 4], BF16, name=f"w1_grp{g}", align_bytes=64)
-            copy = nc.scalar.copy if (e, g) in W1_ON_SCALAR else nc.vector.tensor_copy
-            copy(out=grp[:].rearrange("p t m j -> p m t j"), in_=w1_raw[e, g].rearrange("p j (m t) -> p m t j", t=4))
-            w1_grp[e, g] = grp
+        def copy_w1(e):
+            w1_grp[e] = grouped1.tile([P, 2, 4, 128, 4], BF16, name="w1_grp", align_bytes=64)
+            dst = w1_grp[e][:].rearrange("p g t m j -> p g m t j")
+            parts = len(W1_ENGINES[e])
+            for g in range(parts):
+                if len(w1_raw[e]) == 2:
+                    src = w1_raw[e][g]
+                else:
+                    src = w1_raw[e][0][:, :, g * H // parts:(g + 1) * H // parts]
+                copy_on(W1_ENGINES[e][g], dst[:, g * 2 // parts:(g + 1) * 2 // parts],
+                        src.rearrange("p j (g m t) -> p g m t j", m=128, t=4))
 
-        def quant_w1(e, g):
-            words = codes.tile([P, 512], U32, name=f"w1_words{g}", align_bytes=64)
-            scales = codes.tile([P, 512], U8, name=f"w1_scales{g}", align_bytes=64)
-            nc.vector.quantize_mx(out=words[:].bitcast(FP8X4), scales=scales[:],
-                                  in_=w1_grp[e, g][:].rearrange("p t m j -> p (t m j)"))
-            w1_codes[e, g] = (words, scales)
+        def quant_w1(e, g=None):
+            part = slice(0, 2) if g is None else slice(g, g + 1)
+            cols = slice(part.start * 512, part.stop * 512)
+            if e not in w1_codes:
+                words = w1_pool.tile([P, H], U32, name="w1_words", align_bytes=64)
+                scales = w1_pool.tile([P, H], U8, name="w1_scales", align_bytes=64)
+                w1_codes[e] = (words, scales)
+            words, scales = w1_codes[e]
+            quantize(words[:, cols], scales[:, cols], w1_grp[e][:, part].rearrange("p g t m j -> p (g t m j)"))
 
-        def copy_w2(e):
-            w2_grp[e] = grouped.tile([P, 2, N, 4], BF16, name="w2_grp", align_bytes=64)
-            copy = nc.scalar.copy if e in W2_ON_SCALAR else nc.vector.tensor_copy
-            copy(out=w2_grp[e][:], in_=w2_raw[e][:].rearrange("p g j n -> p g n j"))
+        def copy_w2(i):
+            w2_grp[i] = grouped2.tile([P, 4, N, 4], BF16, name="w2_grp", align_bytes=64)
+            parts = len(W2_ENGINES[i])
+            for q in range(parts):
+                part = slice(q * 4 // parts, (q + 1) * 4 // parts)
+                copy_on(W2_ENGINES[i][q], w2_grp[i][:, part], w2_raw[i][:, part].rearrange("p q j n -> p q n j"))
 
-        def quant_w2(e):
-            words = codes.tile([P, 2 * N], U32, name="w2_words", align_bytes=64)
-            scales = codes.tile([P, 2 * N], U8, name="w2_scales", align_bytes=64)
-            nc.vector.quantize_mx(out=words[:].bitcast(FP8X4), scales=scales[:],
-                                  in_=w2_grp[e][:].rearrange("p g n j -> p (g n j)"))
-            w2_codes[e] = (words, scales)
+        def quant_w2(i):
+            words = w2_pool.tile([P, 4 * N], U32, name="w2_words", align_bytes=64)
+            scales = w2_pool.tile([P, 4 * N], U8, name="w2_scales", align_bytes=64)
+            quantize(words[:], scales[:], w2_grp[i][:].rearrange("p q n j -> p (q n j)"))
+            w2_codes[i] = (words, scales)
 
         def mm1(e, g):
-            if g == 0:
+            if e not in relu_sb:
                 relu_sb[e] = hidden.tile([P, 2, C, 4], F32, name="relu")
                 h_grp[e] = hidden.tile([P, 2, C, 4], BF16, name="h_grp", align_bytes=64)
-            words, scales = w1_codes[e, g]
+            words, scales = w1_codes[e]
             slot_words, slot_scales, first = slot_codes[e]
             for s in range(2):
                 acc = psum1.tile([P, 4, 128], F32, name="acc1")
                 cols = slice(first + s * 128, first + (s + 1) * 128)
                 for t in range(4):
-                    rows = slice(t * 128, (t + 1) * 128)
+                    rows = slice((g * 4 + t) * 128, (g * 4 + t + 1) * 128)
                     nc.tensor.matmul_mx(out=acc[:, t, :],
                                         lhsT=words[:, rows].bitcast(FP8X4), lhsT_scale=scales[:, rows],
                                         rhs=slot_words[:, cols].bitcast(FP8X4), rhs_scale=slot_scales[:, cols],
                                         start=True, stop=True)
                 dst, src = relu_sb[e][:, g, s * 128:(s + 1) * 128, :], acc[:].rearrange("p t c -> p c t")
-                nc.scalar.activation(out=dst, in_=src, func=RELU)
+                if (e, g, s) in VECTOR_RELU:
+                    nc.vector.tensor_scalar_max(dst, src, 0.0)
+                else:
+                    nc.scalar.activation(out=dst, in_=src, func=RELU)
 
         def square(e, g=None):
             part = slice(0, 2) if g is None else slice(g, g + 1)
-            nc.scalar.activation(out=h_grp[e][:, part, :, :], in_=relu_sb[e][:, part, :, :], func=SQUARE)
+            nc.scalar.activation(out=h_grp[e][:, part], in_=relu_sb[e][:, part], func=SQUARE)
 
         def quant_h(e, g=None):
             part = slice(0, 2) if g is None else slice(g, g + 1)
             cols = slice(part.start * C, part.stop * C)
             if e not in h_codes:
-                words = codes.tile([P, 2 * C], U32, name="h_words", align_bytes=64)
-                scales = codes.tile([P, 2 * C], U8, name="h_scales", align_bytes=64)
+                words = hcodes.tile([P, 2 * C], U32, name="h_words", align_bytes=64)
+                scales = hcodes.tile([P, 2 * C], U8, name="h_scales", align_bytes=64)
                 h_codes[e] = (words, scales)
             words, scales = h_codes[e]
-            nc.vector.quantize_mx(out=words[:, cols].bitcast(FP8X4), scales=scales[:, cols],
-                                  in_=h_grp[e][:, part, :, :].rearrange("p g c t -> p (g c t)"))
+            quantize(words[:, cols], scales[:, cols], h_grp[e][:, part].rearrange("p g c t -> p (g c t)"))
 
-        def mm2(e):
-            acc = psum2.tile([P, 2, C], F32, name="acc2")
-            w_words, w_scales = w2_codes[e]
-            h_words, h_scales = h_codes[e]
+        def mm2(*experts):
             for b in range(2):
-                for g in range(2):
-                    rows = slice(g * N + b * 128, g * N + (b + 1) * 128)
-                    cols = slice(g * C, (g + 1) * C)
-                    nc.tensor.matmul_mx(out=acc[:, b, :],
-                                        lhsT=w_words[:, rows].bitcast(FP8X4), lhsT_scale=w_scales[:, rows],
-                                        rhs=h_words[:, cols].bitcast(FP8X4), rhs_scale=h_scales[:, cols],
-                                        start=(g == 0), stop=(g == 1))
-                copy = nc.scalar.copy if Y_ENGINES[e][b] == "S" else nc.vector.tensor_copy
-                copy(out=y_sb[b][:, e * C:(e + 1) * C], in_=acc[:, b, :])
+                acc = psum2.tile([P, 2, C], F32, name="acc2")
+                for i, e in enumerate(experts):
+                    w_words, w_scales = w2_codes[e // 2]
+                    h_words, h_scales = h_codes[e]
+                    for g in range(2):
+                        first = (e % 2 * 2 + g) * N + b * 128
+                        rows, cols = slice(first, first + 128), slice(g * C, (g + 1) * C)
+                        nc.tensor.matmul_mx(out=acc[:, i, :],
+                                            lhsT=w_words[:, rows].bitcast(FP8X4), lhsT_scale=w_scales[:, rows],
+                                            rhs=h_words[:, cols].bitcast(FP8X4), rhs_scale=h_scales[:, cols],
+                                            start=(g == 0), stop=(g == 1))
+                n = len(experts)
+                copy_on(Y_ENGINES[experts[0]][b], y_sb[b][:, experts[0] * C:(experts[0] + n) * C],
+                        acc[:, :n, :].rearrange("p e c -> p (e c)"))
 
         def combine(b):
             terms = []
@@ -180,60 +207,83 @@ def tile_routed_moe_kernel(tc, xT, w1, w2, gate, offs, pos1, pos2, out):
             nc.vector.tensor_tensor(out=res[:], in0=terms[0][:], in1=terms[1][:], op=ADD)
             nc.sync.dma_start(out[b * 128:(b + 1) * 128, :], res[:])
 
-        load_offs()
+        load_x(2)
         load_x(0)
+        load_offs()
         load_x(1)
+        copy_x(1, "B")
         load_w1_half(0, 0)
         load_w1_half(0, 1)
         load_w1(1)
-        load_w2(0)
-        load_w1(2)
-        copy_x(0)
-        copy_x(1)
+        copy_x(0, "B")
         quant_x(0)
-        quant_x(1)
-        copy_w1(0, 0)
+        copy_x(2, "B")
+        copy_w1(0)
         quant_w1(0, 0)
-        gather(0, 1)
-        for e in range(E):
-            if e > 0:
-                copy_w1(e, 0)
-            copy_w1(e, 1)
-            if e + 3 < E:
-                load_w1(e + 3)
-            if e == 1:
-                load_pos()
-            if e < 3:
-                load_w2(e + 1)
-            if e == 3:
-                load_w2(4)
-            if e == 4:
-                load_w2(5)
-                load_gate(0)
-                load_gate(1)
-            if e in (1, 3):
-                gather(e, e + 2)
-            if e == 5:
-                gather(5, 6)
-            if e > 0:
-                quant_w1(e, 0)
-            mm1(e, 0)
-            if e > 1:
-                mm2(e - 2)
-            if e > 0:
-                quant_h(e - 1)
-            quant_w1(e, 1)
-            mm1(e, 1)
-            if e < 5:
-                square(e)
-            else:
-                square(e, 0)
-                square(e, 1)
-            copy_w2(e)
-            quant_w2(e)
-        mm2(4)
-        quant_h(5, 0)
-        quant_h(5, 1)
-        mm2(5)
-        combine(0)
+        copy_w1(1)
+        quant_x(2)
+        load_w1(2)
+        load_w1(5)
+        quant_x(1)
+        gather(0, 2)
+        quant_w1(1, 1)
+        load_w1(4)
+        copy_w1(2)
+        gather(4, 6)
+        quant_w1(0, 1)
+        mm1(0, 1)
+        quant_w1(2)
+        mm1(0, 0)
+        quant_w1(1, 0)
+        copy_w1(4)
+        copy_w1(5)
+        mm1(1, 0)
+        load_w2(0)
+        copy_w2(0)
+        quant_w1(4, 1)
+        load_w2(2)
+        quant_w1(4, 0)
+        mm1(1, 1)
+        quant_w1(5)
+        square(1)
+        load_w1(3)
+        square(0)
+        quant_h(0)
+        mm1(4, 1)
+        copy_w1(3)
+        mm1(4, 0)
+        load_w2(1)
+        quant_h(1, 1)
+        load_gate(0)
+        quant_h(1, 0)
+        load_pos()
+        quant_w2(0)
+        load_gate(1)
+        gather(2, 4)
+        square(4)
+        quant_w1(3)
+        mm1(2, 1)
+        mm1(2, 0)
+        quant_h(4)
+        square(2)
+        mm1(5, 0)
+        copy_w2(2)
+        mm1(5, 1)
+        mm2(0, 1)
+        quant_h(2)
+        square(5)
+        quant_w2(2)
+        quant_h(5)
+        copy_w2(1)
+        mm1(3, 1)
+        square(3, 1)
+        quant_w2(1)
+        mm2(4, 5)
+        mm2(2)
+        mm1(3, 0)
+        square(3, 0)
+        quant_h(3, 1)
+        quant_h(3, 0)
+        mm2(3)
         combine(1)
+        combine(0)

@@ -16,11 +16,11 @@ SQUARE = mybir.ActivationFunctionType.Square
 MULT, ADD = mybir.AluOpType.mult, mybir.AluOpType.add
 
 P = 128
-X_CHUNK = 256
-W1_ENGINES = ["SS","VV","V","V","SS","VS"]
-W2_ENGINES = ["V","V","V"]
-VECTOR_RELU = ((2, 1, 0), (2, 1, 1), (1, 1, 0), (1, 1, 1), (3, 1, 1), (1, 0, 0), )
-Y_ENGINES = ["SS","VS","SV","SS","SS","VV"]
+X_CHUNKS = ((0, 512), (512, 768))
+W1_ENGINES = ["SV","V","SS","V","VV","V"]
+W2_ENGINES = ["SV","VS","VV"]
+VECTOR_RELU = ((4, 0, 0), (1, 0, 0), (5, 1, 1), )
+Y_ENGINES = ["SV","SV","VS","SS","SS","SS"]
 
 
 def tile_routed_moe_kernel(tc, xT, w1, w2, gate, offs, pos1, pos2, out):
@@ -28,12 +28,12 @@ def tile_routed_moe_kernel(tc, xT, w1, w2, gate, offs, pos1, pos2, out):
     with ExitStack() as ctx:
         keep = ctx.enter_context(tc.tile_pool(name="keep", bufs=1))
         raws = ctx.enter_context(tc.tile_pool(name="raws", bufs=3))
-        grouped1 = ctx.enter_context(tc.tile_pool(name="grouped1", bufs=3))
-        grouped2 = ctx.enter_context(tc.tile_pool(name="grouped2", bufs=1))
-        w1_pool = ctx.enter_context(tc.tile_pool(name="w1_pool", bufs=4))
+        grouped1 = ctx.enter_context(tc.tile_pool(name="grouped1", bufs=2))
+        grouped2 = ctx.enter_context(tc.tile_pool(name="grouped2", bufs=2))
+        w1_pool = ctx.enter_context(tc.tile_pool(name="w1_pool", bufs=2))
         w2_pool = ctx.enter_context(tc.tile_pool(name="w2_pool", bufs=3))
-        slots = ctx.enter_context(tc.tile_pool(name="slots", bufs=3))
-        hcodes = ctx.enter_context(tc.tile_pool(name="hcodes", bufs=3))
+        slots = ctx.enter_context(tc.tile_pool(name="slots", bufs=6))
+        hcodes = ctx.enter_context(tc.tile_pool(name="hcodes", bufs=6))
         hidden = ctx.enter_context(tc.tile_pool(name="hidden", bufs=2))
         results = ctx.enter_context(tc.tile_pool(name="results", bufs=2))
         psum1 = ctx.enter_context(tc.psum_pool(name="psum1", bufs=6))
@@ -41,7 +41,7 @@ def tile_routed_moe_kernel(tc, xT, w1, w2, gate, offs, pos1, pos2, out):
 
         offs_sb = keep.tile([P, E * C // 16], U16, name="offs_sb")
         pos_sb = [keep.tile([P, T // 16], U16, name=f"pos{r}_sb") for r in range(2)]
-        x_raw = [keep.tile([P, 4, X_CHUNK], F32, name=f"x_raw{i}") for i in range(3)]
+        x_raw = keep.tile([P, 4, T], F32, name="x_raw")
         x_words = keep.tile([P, T], U32, name="x_words", align_bytes=64)
         x_scales = keep.tile([P, T], U8, name="x_scales", align_bytes=64)
         gate_sb = [[keep.tile([P, T], F32, name=f"gate{r}{b}") for b in range(2)] for r in range(2)]
@@ -66,7 +66,7 @@ def tile_routed_moe_kernel(tc, xT, w1, w2, gate, offs, pos1, pos2, out):
                 nc.sync.dma_start(pos_sb[r][:], src)
 
         def load_x(i):
-            nc.sync.dma_start(x_raw[i][:], xT.rearrange("(p j) t -> p j t", j=4)[:, :, i * X_CHUNK:(i + 1) * X_CHUNK])
+            nc.sync.dma_start(x_raw[:], xT.rearrange("(p j) t -> p j t", j=4))
 
         def load_w1(e):
             raw = raws.tile([P, 4, H], F32, name="raw")
@@ -87,17 +87,19 @@ def tile_routed_moe_kernel(tc, xT, w1, w2, gate, offs, pos1, pos2, out):
                 nc.sync.dma_start(gate_sb[r][b][:], gate[r, b * 128:(b + 1) * 128, :])
 
         def copy_x(i, how):
-            x_grp[i] = keep.tile([P, X_CHUNK, 4], BF16, name=f"x_grp{i}", align_bytes=64)
-            src = x_raw[i][:].rearrange("p j t -> p t j")
+            a, b = X_CHUNKS[i]
+            x_grp[i] = keep.tile([P, b - a, 4], BF16, name=f"x_grp{i}", align_bytes=64)
+            dst = x_grp[i][:].rearrange("p (c i) j -> p c j i", i=4)
+            src = x_raw[:, :, a:b].rearrange("p j (c i) -> p c j i", i=4)
             if how == "B":
-                half = X_CHUNK // 2
-                copy_on("V", x_grp[i][:, :half, :], src[:, :half, :])
-                copy_on("S", x_grp[i][:, half:, :], src[:, half:, :])
+                half = (b - a) // 8
+                copy_on("V", dst[:, :half], src[:, :half])
+                copy_on("S", dst[:, half:], src[:, half:])
             else:
-                copy_on(how, x_grp[i][:], src)
+                copy_on(how, dst, src)
 
         def quant_x(i):
-            cols = slice(i * X_CHUNK, (i + 1) * X_CHUNK)
+            cols = slice(*X_CHUNKS[i])
             quantize(x_words[:, cols], x_scales[:, cols], x_grp[i][:].rearrange("p t j -> p (t j)"))
 
         def gather(e0, e1):
@@ -112,7 +114,7 @@ def tile_routed_moe_kernel(tc, xT, w1, w2, gate, offs, pos1, pos2, out):
 
         def copy_w1(e):
             w1_grp[e] = grouped1.tile([P, 2, 4, 128, 4], BF16, name="w1_grp", align_bytes=64)
-            dst = w1_grp[e][:].rearrange("p g t m j -> p g m t j")
+            dst = w1_grp[e][:].rearrange("p g t m j -> p g m j t")
             parts = len(W1_ENGINES[e])
             for g in range(parts):
                 if len(w1_raw[e]) == 2:
@@ -120,7 +122,7 @@ def tile_routed_moe_kernel(tc, xT, w1, w2, gate, offs, pos1, pos2, out):
                 else:
                     src = w1_raw[e][0][:, :, g * H // parts:(g + 1) * H // parts]
                 copy_on(W1_ENGINES[e][g], dst[:, g * 2 // parts:(g + 1) * 2 // parts],
-                        src.rearrange("p j (g m t) -> p g m t j", m=128, t=4))
+                        src.rearrange("p j (g m t) -> p g m j t", m=128, t=4))
 
         def quant_w1(e, g=None):
             part = slice(0, 2) if g is None else slice(g, g + 1)
@@ -138,6 +140,27 @@ def tile_routed_moe_kernel(tc, xT, w1, w2, gate, offs, pos1, pos2, out):
             for q in range(parts):
                 part = slice(q * 4 // parts, (q + 1) * 4 // parts)
                 copy_on(W2_ENGINES[i][q], w2_grp[i][:, part], w2_raw[i][:, part].rearrange("p q j n -> p q n j"))
+
+        def load_w2_half(i, q):
+            if i not in w2_raw:
+                w2_raw[i] = raws.tile([P, 4, 4, N], F32, name="raw")
+            nc.sync.dma_start(w2_raw[i][:, 2 * q:2 * q + 2], w2[2 * i + q].rearrange("(g p j) n -> p g j n", g=2, j=4))
+
+        def copy_w2_half(i, q):
+            if i not in w2_grp:
+                w2_grp[i] = grouped2.tile([P, 4, N, 4], BF16, name="w2_grp", align_bytes=64)
+            part = slice(2 * q, 2 * q + 2)
+            copy_on(W2_ENGINES[i][q], w2_grp[i][:, part].rearrange("p q (c i) j -> p q c j i", i=4),
+                    w2_raw[i][:, part].rearrange("p q j (c i) -> p q c j i", i=4))
+
+        def quant_w2_half(i, q):
+            if i not in w2_codes:
+                words = w2_pool.tile([P, 4 * N], U32, name="w2_words", align_bytes=64)
+                scales = w2_pool.tile([P, 4 * N], U8, name="w2_scales", align_bytes=64)
+                w2_codes[i] = (words, scales)
+            words, scales = w2_codes[i]
+            cols = slice(2 * q * N, (2 * q + 2) * N)
+            quantize(words[:, cols], scales[:, cols], w2_grp[i][:, 2 * q:2 * q + 2].rearrange("p q n j -> p (q n j)"))
 
         def quant_w2(i):
             words = w2_pool.tile([P, 4 * N], U32, name="w2_words", align_bytes=64)
@@ -198,92 +221,96 @@ def tile_routed_moe_kernel(tc, xT, w1, w2, gate, offs, pos1, pos2, out):
                         acc[:, :n, :].rearrange("p e c -> p (e c)"))
 
         def combine(b):
-            terms = []
-            for r in range(2):
-                term = results.tile([P, T], F32, name=f"term{r}")
-                nc.vector.tensor_tensor(out=term[:], in0=y_sb[b][:].indirect(pos_sb[r][:]), in1=gate_sb[r][b][:], op=MULT)
-                terms.append(term)
+            terms = [results.tile([P, T], F32, name=f"term{r}") for r in range(2)]
             res = results.tile([P, T], F32, name="res")
-            nc.vector.tensor_tensor(out=res[:], in0=terms[0][:], in1=terms[1][:], op=ADD)
-            nc.sync.dma_start(out[b * 128:(b + 1) * 128, :], res[:])
+            for c0, c1 in ([0,512],[512,768]) if b == 1 else ((0, T),):
+                for r in range(2):
+                    nc.vector.tensor_tensor(out=terms[r][:, c0:c1], in0=y_sb[b][:].indirect(pos_sb[r][:, c0 // 16:c1 // 16]),
+                                            in1=gate_sb[r][b][:, c0:c1], op=MULT)
+                nc.vector.tensor_tensor(out=res[:, c0:c1], in0=terms[0][:, c0:c1], in1=terms[1][:, c0:c1], op=ADD)
+                nc.sync.dma_start(out[b * 128:(b + 1) * 128, c0:c1], res[:, c0:c1])
 
-        load_x(2)
-        load_x(0)
         load_offs()
-        load_x(1)
-        copy_x(1, "B")
-        load_w1_half(0, 0)
-        load_w1_half(0, 1)
-        load_w1(1)
-        copy_x(0, "B")
-        quant_x(0)
-        copy_x(2, "B")
-        copy_w1(0)
-        quant_w1(0, 0)
-        copy_w1(1)
-        quant_x(2)
+        load_x(0)
         load_w1(2)
-        load_w1(5)
-        quant_x(1)
-        gather(0, 2)
-        quant_w1(1, 1)
-        load_w1(4)
-        copy_w1(2)
-        gather(4, 6)
-        quant_w1(0, 1)
-        mm1(0, 1)
-        quant_w1(2)
-        mm1(0, 0)
-        quant_w1(1, 0)
-        copy_w1(4)
-        copy_w1(5)
-        mm1(1, 0)
-        load_w2(0)
-        copy_w2(0)
-        quant_w1(4, 1)
-        load_w2(2)
-        quant_w1(4, 0)
-        mm1(1, 1)
-        quant_w1(5)
-        square(1)
         load_w1(3)
-        square(0)
-        quant_h(0)
-        mm1(4, 1)
-        copy_w1(3)
-        mm1(4, 0)
-        load_w2(1)
-        quant_h(1, 1)
-        load_gate(0)
-        quant_h(1, 0)
-        load_pos()
-        quant_w2(0)
-        load_gate(1)
+        copy_x(0, "B")
+        copy_x(1, "B")
+        quant_x(0)
+        quant_x(1)
         gather(2, 4)
-        square(4)
-        quant_w1(3)
-        mm1(2, 1)
+        gather(4, 6)
+        load_w1(5)
+        copy_w1(2)
+        quant_w1(2, 0)
         mm1(2, 0)
-        quant_h(4)
+        quant_w1(2, 1)
+        mm1(2, 1)
         square(2)
-        mm1(5, 0)
-        copy_w2(2)
-        mm1(5, 1)
-        mm2(0, 1)
-        quant_h(2)
-        square(5)
-        quant_w2(2)
-        quant_h(5)
-        copy_w2(1)
-        mm1(3, 1)
-        square(3, 1)
-        quant_w2(1)
-        mm2(4, 5)
-        mm2(2)
+        load_w1(4)
+        copy_w1(3)
+        quant_w1(3)
         mm1(3, 0)
-        square(3, 0)
-        quant_h(3, 1)
-        quant_h(3, 0)
+        mm1(3, 1)
+        square(3)
+        load_w2_half(1, 1)
+        quant_h(2)
+        copy_w1(5)
+        quant_w1(5, 0)
+        mm1(5, 0)
+        quant_w1(5, 1)
+        mm1(5, 1)
+        square(5)
+        load_w2_half(1, 0)
+        quant_h(3)
+        copy_w1(4)
+        quant_w1(4)
+        mm1(4, 0)
+        mm1(4, 1)
+        square(4)
+        load_w2_half(2, 0)
+        quant_h(5)
+        copy_w2_half(1, 1)
+        quant_w2_half(1, 1)
         mm2(3)
-        combine(1)
+        load_w1_half(0, 0)
+        copy_w2_half(1, 0)
+        quant_w2_half(1, 0)
+        mm2(2)
+        load_w1(1)
+        quant_h(4)
+        copy_w2_half(2, 0)
+        quant_w2_half(2, 0)
+        mm2(4)
+        load_w2_half(0, 0)
+        load_w1_half(0, 1)
+        copy_w1(1)
+        gather(0, 2)
+        quant_w1(1, 0)
+        mm1(1, 0)
+        quant_w1(1, 1)
+        mm1(1, 1)
+        square(1)
+        load_w2_half(0, 1)
+        copy_w2_half(0, 0)
+        quant_w2_half(0, 0)
+        load_w2_half(2, 1)
+        quant_h(1)
+        copy_w1(0)
+        quant_w1(0)
+        mm1(0, 0)
+        mm1(0, 1)
+        square(0)
+        load_pos()
+        copy_w2_half(0, 1)
+        quant_w2_half(0, 1)
+        mm2(1)
+        load_gate(1)
+        copy_w2_half(2, 1)
+        quant_w2_half(2, 1)
+        mm2(5)
+        load_gate(0)
+        quant_h(0)
+        mm2(0)
         combine(0)
+        combine(1)

from contextlib import ExitStack

import concourse.mybir as mybir

K, T, E, C, H, N = 512, 768, 6, 256, 1024, 256
FLOPS = 2 * E * C * (K * H + H * N)

F32 = mybir.dt.float32
BF16 = mybir.dt.bfloat16
U32 = mybir.dt.uint32
U16 = mybir.dt.uint16
U8 = mybir.dt.uint8
FP8X4 = mybir.dt.float8_e4m3fn_x4
RELU = mybir.ActivationFunctionType.Relu
SQUARE = mybir.ActivationFunctionType.Square
MULT, ADD = mybir.AluOpType.mult, mybir.AluOpType.add

P = 128
X_CHUNKS = ((0, 512), (512, 768))
W1_ENGINES = ["SV","V","SS","V","VV","V"]
W2_ENGINES = ["SV","VS","VV"]
VECTOR_RELU = ((4, 0, 0), (1, 0, 0), (5, 1, 1), )
Y_ENGINES = ["SV","SV","VS","SS","SS","SS"]


def tile_routed_moe_kernel(tc, xT, w1, w2, gate, offs, pos1, pos2, out):
    nc = tc.nc
    with ExitStack() as ctx:
        keep = ctx.enter_context(tc.tile_pool(name="keep", bufs=1))
        raws = ctx.enter_context(tc.tile_pool(name="raws", bufs=3))
        grouped1 = ctx.enter_context(tc.tile_pool(name="grouped1", bufs=2))
        grouped2 = ctx.enter_context(tc.tile_pool(name="grouped2", bufs=2))
        w1_pool = ctx.enter_context(tc.tile_pool(name="w1_pool", bufs=2))
        w2_pool = ctx.enter_context(tc.tile_pool(name="w2_pool", bufs=3))
        slots = ctx.enter_context(tc.tile_pool(name="slots", bufs=6))
        hcodes = ctx.enter_context(tc.tile_pool(name="hcodes", bufs=6))
        hidden = ctx.enter_context(tc.tile_pool(name="hidden", bufs=2))
        results = ctx.enter_context(tc.tile_pool(name="results", bufs=2))
        psum1 = ctx.enter_context(tc.psum_pool(name="psum1", bufs=6))
        psum2 = ctx.enter_context(tc.psum_pool(name="psum2", bufs=2))

        offs_sb = keep.tile([P, E * C // 16], U16, name="offs_sb")
        pos_sb = [keep.tile([P, T // 16], U16, name=f"pos{r}_sb") for r in range(2)]
        x_raw = keep.tile([P, 4, T], F32, name="x_raw")
        x_words = keep.tile([P, T], U32, name="x_words", align_bytes=64)
        x_scales = keep.tile([P, T], U8, name="x_scales", align_bytes=64)
        gate_sb = [[keep.tile([P, T], F32, name=f"gate{r}{b}") for b in range(2)] for r in range(2)]
        y_sb = [keep.tile([P, E * C], F32, name=f"y{b}") for b in range(2)]
        w1_raw, w2_raw, w1_grp, w2_grp, w1_codes, w2_codes = {}, {}, {}, {}, {}, {}
        x_grp, slot_codes, relu_sb, h_grp, h_codes = {}, {}, {}, {}, {}

        def copy_on(engine, dst, src):
            if engine == "S":
                nc.scalar.copy(out=dst, in_=src)
            else:
                nc.vector.tensor_copy(out=dst, in_=src)

        def quantize(words, scales, src):
            nc.vector.quantize_mx(out=words.bitcast(FP8X4), scales=scales, in_=src)

        def load_offs():
            nc.sync.dma_start(offs_sb[:], offs)

        def load_pos():
            for r, src in enumerate((pos1, pos2)):
                nc.sync.dma_start(pos_sb[r][:], src)

        def load_x(i):
            nc.sync.dma_start(x_raw[:], xT.rearrange("(p j) t -> p j t", j=4))

        def load_w1(e):
            raw = raws.tile([P, 4, H], F32, name="raw")
            nc.sync.dma_start(raw[:], w1[e].rearrange("(p j) c -> p j c", j=4))
            w1_raw[e] = [raw[:]]

        def load_w1_half(e, g):
            raw = keep.tile([P, 4, 512], F32, name=f"w1_half{g}")
            nc.sync.dma_start(raw[:], w1[e].rearrange("(p j) c -> p j c", j=4)[:, :, g * 512:(g + 1) * 512])
            w1_raw.setdefault(e, []).append(raw[:])

        def load_w2(i):
            w2_raw[i] = raws.tile([P, 4, 4, N], F32, name="raw")
            nc.sync.dma_start(w2_raw[i][:], w2[2 * i:2 * i + 2].rearrange("e (g p j) n -> p (e g) j n", g=2, j=4))

        def load_gate(b):
            for r in range(2):
                nc.sync.dma_start(gate_sb[r][b][:], gate[r, b * 128:(b + 1) * 128, :])

        def copy_x(i, how):
            a, b = X_CHUNKS[i]
            x_grp[i] = keep.tile([P, b - a, 4], BF16, name=f"x_grp{i}", align_bytes=64)
            dst = x_grp[i][:].rearrange("p (c i) j -> p c j i", i=4)
            src = x_raw[:, :, a:b].rearrange("p j (c i) -> p c j i", i=4)
            if how == "B":
                half = (b - a) // 8
                copy_on("V", dst[:, :half], src[:, :half])
                copy_on("S", dst[:, half:], src[:, half:])
            else:
                copy_on(how, dst, src)

        def quant_x(i):
            cols = slice(*X_CHUNKS[i])
            quantize(x_words[:, cols], x_scales[:, cols], x_grp[i][:].rearrange("p t j -> p (t j)"))

        def gather(e0, e1):
            n = (e1 - e0) * C
            o = offs_sb[:, e0 * C // 16:e1 * C // 16]
            words = slots.tile([P, n], U32, name="slot_words", align_bytes=64)
            scales = slots.tile([P, n], U8, name="slot_scales", align_bytes=64)
            nc.vector.tensor_copy(out=words[:], in_=x_words[:].indirect(o))
            nc.vector.tensor_copy(out=scales[:], in_=x_scales[:].indirect(o))
            for e in range(e0, e1):
                slot_codes[e] = (words, scales, (e - e0) * C)

        def copy_w1(e):
            w1_grp[e] = grouped1.tile([P, 2, 4, 128, 4], BF16, name="w1_grp", align_bytes=64)
            dst = w1_grp[e][:].rearrange("p g t m j -> p g m j t")
            parts = len(W1_ENGINES[e])
            for g in range(parts):
                if len(w1_raw[e]) == 2:
                    src = w1_raw[e][g]
                else:
                    src = w1_raw[e][0][:, :, g * H // parts:(g + 1) * H // parts]
                copy_on(W1_ENGINES[e][g], dst[:, g * 2 // parts:(g + 1) * 2 // parts],
                        src.rearrange("p j (g m t) -> p g m j t", m=128, t=4))

        def quant_w1(e, g=None):
            part = slice(0, 2) if g is None else slice(g, g + 1)
            cols = slice(part.start * 512, part.stop * 512)
            if e not in w1_codes:
                words = w1_pool.tile([P, H], U32, name="w1_words", align_bytes=64)
                scales = w1_pool.tile([P, H], U8, name="w1_scales", align_bytes=64)
                w1_codes[e] = (words, scales)
            words, scales = w1_codes[e]
            quantize(words[:, cols], scales[:, cols], w1_grp[e][:, part].rearrange("p g t m j -> p (g t m j)"))

        def copy_w2(i):
            w2_grp[i] = grouped2.tile([P, 4, N, 4], BF16, name="w2_grp", align_bytes=64)
            parts = len(W2_ENGINES[i])
            for q in range(parts):
                part = slice(q * 4 // parts, (q + 1) * 4 // parts)
                copy_on(W2_ENGINES[i][q], w2_grp[i][:, part], w2_raw[i][:, part].rearrange("p q j n -> p q n j"))

        def load_w2_half(i, q):
            if i not in w2_raw:
                w2_raw[i] = raws.tile([P, 4, 4, N], F32, name="raw")
            nc.sync.dma_start(w2_raw[i][:, 2 * q:2 * q + 2], w2[2 * i + q].rearrange("(g p j) n -> p g j n", g=2, j=4))

        def copy_w2_half(i, q):
            if i not in w2_grp:
                w2_grp[i] = grouped2.tile([P, 4, N, 4], BF16, name="w2_grp", align_bytes=64)
            part = slice(2 * q, 2 * q + 2)
            copy_on(W2_ENGINES[i][q], w2_grp[i][:, part].rearrange("p q (c i) j -> p q c j i", i=4),
                    w2_raw[i][:, part].rearrange("p q j (c i) -> p q c j i", i=4))

        def quant_w2_half(i, q):
            if i not in w2_codes:
                words = w2_pool.tile([P, 4 * N], U32, name="w2_words", align_bytes=64)
                scales = w2_pool.tile([P, 4 * N], U8, name="w2_scales", align_bytes=64)
                w2_codes[i] = (words, scales)
            words, scales = w2_codes[i]
            cols = slice(2 * q * N, (2 * q + 2) * N)
            quantize(words[:, cols], scales[:, cols], w2_grp[i][:, 2 * q:2 * q + 2].rearrange("p q n j -> p (q n j)"))

        def quant_w2(i):
            words = w2_pool.tile([P, 4 * N], U32, name="w2_words", align_bytes=64)
            scales = w2_pool.tile([P, 4 * N], U8, name="w2_scales", align_bytes=64)
            quantize(words[:], scales[:], w2_grp[i][:].rearrange("p q n j -> p (q n j)"))
            w2_codes[i] = (words, scales)

        def mm1(e, g):
            if e not in relu_sb:
                relu_sb[e] = hidden.tile([P, 2, C, 4], F32, name="relu")
                h_grp[e] = hidden.tile([P, 2, C, 4], BF16, name="h_grp", align_bytes=64)
            words, scales = w1_codes[e]
            slot_words, slot_scales, first = slot_codes[e]
            for s in range(2):
                acc = psum1.tile([P, 4, 128], F32, name="acc1")
                cols = slice(first + s * 128, first + (s + 1) * 128)
                for t in range(4):
                    rows = slice((g * 4 + t) * 128, (g * 4 + t + 1) * 128)
                    nc.tensor.matmul_mx(out=acc[:, t, :],
                                        lhsT=words[:, rows].bitcast(FP8X4), lhsT_scale=scales[:, rows],
                                        rhs=slot_words[:, cols].bitcast(FP8X4), rhs_scale=slot_scales[:, cols],
                                        start=True, stop=True)
                dst, src = relu_sb[e][:, g, s * 128:(s + 1) * 128, :], acc[:].rearrange("p t c -> p c t")
                if (e, g, s) in VECTOR_RELU:
                    nc.vector.tensor_scalar_max(dst, src, 0.0)
                else:
                    nc.scalar.activation(out=dst, in_=src, func=RELU)

        def square(e, g=None):
            part = slice(0, 2) if g is None else slice(g, g + 1)
            nc.scalar.activation(out=h_grp[e][:, part], in_=relu_sb[e][:, part], func=SQUARE)

        def quant_h(e, g=None):
            part = slice(0, 2) if g is None else slice(g, g + 1)
            cols = slice(part.start * C, part.stop * C)
            if e not in h_codes:
                words = hcodes.tile([P, 2 * C], U32, name="h_words", align_bytes=64)
                scales = hcodes.tile([P, 2 * C], U8, name="h_scales", align_bytes=64)
                h_codes[e] = (words, scales)
            words, scales = h_codes[e]
            quantize(words[:, cols], scales[:, cols], h_grp[e][:, part].rearrange("p g c t -> p (g c t)"))

        def mm2(*experts):
            for b in range(2):
                acc = psum2.tile([P, 2, C], F32, name="acc2")
                for i, e in enumerate(experts):
                    w_words, w_scales = w2_codes[e // 2]
                    h_words, h_scales = h_codes[e]
                    for g in range(2):
                        first = (e % 2 * 2 + g) * N + b * 128
                        rows, cols = slice(first, first + 128), slice(g * C, (g + 1) * C)
                        nc.tensor.matmul_mx(out=acc[:, i, :],
                                            lhsT=w_words[:, rows].bitcast(FP8X4), lhsT_scale=w_scales[:, rows],
                                            rhs=h_words[:, cols].bitcast(FP8X4), rhs_scale=h_scales[:, cols],
                                            start=(g == 0), stop=(g == 1))
                n = len(experts)
                copy_on(Y_ENGINES[experts[0]][b], y_sb[b][:, experts[0] * C:(experts[0] + n) * C],
                        acc[:, :n, :].rearrange("p e c -> p (e c)"))

        def combine(b):
            terms = [results.tile([P, T], F32, name=f"term{r}") for r in range(2)]
            res = results.tile([P, T], F32, name="res")
            for c0, c1 in ([0,512],[512,768]) if b == 1 else ((0, T),):
                for r in range(2):
                    nc.vector.tensor_tensor(out=terms[r][:, c0:c1], in0=y_sb[b][:].indirect(pos_sb[r][:, c0 // 16:c1 // 16]),
                                            in1=gate_sb[r][b][:, c0:c1], op=MULT)
                nc.vector.tensor_tensor(out=res[:, c0:c1], in0=terms[0][:, c0:c1], in1=terms[1][:, c0:c1], op=ADD)
                nc.sync.dma_start(out[b * 128:(b + 1) * 128, c0:c1], res[:, c0:c1])

        load_offs()
        load_x(0)
        load_w1(2)
        load_w1(3)
        copy_x(0, "B")
        copy_x(1, "B")
        quant_x(0)
        quant_x(1)
        gather(2, 4)
        gather(4, 6)
        load_w1(5)
        copy_w1(2)
        quant_w1(2, 0)
        mm1(2, 0)
        quant_w1(2, 1)
        mm1(2, 1)
        square(2)
        load_w1(4)
        copy_w1(3)
        quant_w1(3)
        mm1(3, 0)
        mm1(3, 1)
        square(3)
        load_w2_half(1, 1)
        quant_h(2)
        copy_w1(5)
        quant_w1(5, 0)
        mm1(5, 0)
        quant_w1(5, 1)
        mm1(5, 1)
        square(5)
        load_w2_half(1, 0)
        quant_h(3)
        copy_w1(4)
        quant_w1(4)
        mm1(4, 0)
        mm1(4, 1)
        square(4)
        load_w2_half(2, 0)
        quant_h(5)
        copy_w2_half(1, 1)
        quant_w2_half(1, 1)
        mm2(3)
        load_w1_half(0, 0)
        copy_w2_half(1, 0)
        quant_w2_half(1, 0)
        mm2(2)
        load_w1(1)
        quant_h(4)
        copy_w2_half(2, 0)
        quant_w2_half(2, 0)
        mm2(4)
        load_w2_half(0, 0)
        load_w1_half(0, 1)
        copy_w1(1)
        gather(0, 2)
        quant_w1(1, 0)
        mm1(1, 0)
        quant_w1(1, 1)
        mm1(1, 1)
        square(1)
        load_w2_half(0, 1)
        copy_w2_half(0, 0)
        quant_w2_half(0, 0)
        load_w2_half(2, 1)
        quant_h(1)
        copy_w1(0)
        quant_w1(0)
        mm1(0, 0)
        mm1(0, 1)
        square(0)
        load_pos()
        copy_w2_half(0, 1)
        quant_w2_half(0, 1)
        mm2(1)
        load_gate(1)
        copy_w2_half(2, 1)
        quant_w2_half(2, 1)
        mm2(5)
        load_gate(0)
        quant_h(0)
        mm2(0)
        combine(0)
        combine(1)
